import numpy as np
import ml_dtypes

BF16 = ml_dtypes.bfloat16


def bf(x):
    return np.asarray(x, np.float32).astype(BF16)


def f32(x):
    return np.asarray(x, np.float32)


def f64(x):
    return np.asarray(x).astype(np.float64)


def striped(idx):
    return np.tile(idx.reshape(-1, 16).T, (8, 1))


S, K, M, N, D, V = 512, 256, 128, 256, 2, 128


def setup_inputs():
    return {"table": bf(np.random.standard_normal((S, K))), "w": bf(np.random.standard_normal((D, K, M)) / np.sqrt(D * K)), "b": f32(0.5 * np.random.standard_normal((M, 1))), "offs": striped(np.random.permutation(S)[:N])}


def reference(table, w, b, offs):
    idx = offs[:16].T.reshape(-1)
    x = f64(table)[idx].T
    y = sum(f64(w)[t].T @ x[:, t * V : (t + 1) * V] for t in range(D))
    return y + f64(b)

@@ -1,0 +1,58 @@
+import concourse.mybir as mybir
+from concourse.masks import make_identity
+
+BF16, F32, U16 = mybir.dt.bfloat16, mybir.dt.float32, mybir.dt.uint16
+
+P = 128
+NODES = 512
+FEATURES = 256
+ENDS = 2
+EDGES = 128
+OUT_FEATURES = 128
+NODE_BLOCKS = NODES // P
+FEATURE_BLOCKS = FEATURES // P
+OFFSET_COLUMNS = EDGES // 16
+
+FLOPS = 2 * ENDS * FEATURES * OUT_FEATURES * EDGES
+
+
+def tile_gather_matmul_kernel(tc, table, w, b, offs, out):
+    nc = tc.nc
+    with (
+        tc.tile_pool(name="held", bufs=1) as held,
+        tc.psum_pool(name="psum", bufs=1) as psum,
+    ):
+        offsets = held.tile([P, ENDS * OFFSET_COLUMNS], U16, name="offsets")
+        nc.sync.dma_start(offsets[:], offs)
+        nodes_first = held.tile([P, NODE_BLOCKS, FEATURES], BF16, name="nodes_first")
+        nc.sync.dma_start(nodes_first[:], table.rearrange("(a p) k -> p a k", p=P))
+        weights = held.tile([P, ENDS, FEATURE_BLOCKS, OUT_FEATURES], BF16, name="weights")
+        nc.scalar.dma_start(weights[:], w.rearrange("t (c p) m -> p t c m", p=P))
+        bias = held.tile([P, 1], F32, name="bias")
+        nc.scalar.dma_start(bias[:], b)
+
+        identity = held.tile([P, P], BF16, name="identity")
+        make_identity(nc, identity[:])
+
+        windows = []
+        for c in range(FEATURE_BLOCKS):
+            flipped = psum.tile([P, NODES], BF16, name=f"flipped{c}")
+            for a in range(NODE_BLOCKS):
+                nc.tensor.transpose(
+                    flipped[:, a * P : (a + 1) * P], nodes_first[:, a, c * P : (c + 1) * P], identity[:]
+                )
+            window = held.tile([P, NODES], BF16, name=f"window{c}")
+            nc.vector.tensor_copy(window[:], flipped[:])
+            windows.append(window)
+
+        product = psum.tile([P, EDGES], F32, name="product")
+        steps = [(c, t) for c in range(FEATURE_BLOCKS) for t in range(ENDS)]
+        for step, (c, t) in enumerate(steps):
+            picked = windows[c][:].indirect(offsets[:, t * OFFSET_COLUMNS : (t + 1) * OFFSET_COLUMNS])
+            nc.tensor.matmul(
+                product[:], weights[:, t, c, :], picked, start=(step == 0), stop=(step == len(steps) - 1)
+            )
+
+        result = held.tile([P, EDGES], F32, name="result")
+        nc.vector.tensor_scalar_add(result[:], product[:], bias[:, 0:1])
+        nc.sync.dma_start(out, result[:])

@@ -11,6 +11,9 @@ EDGES = 128
 OUT_FEATURES = 128
 NODE_BLOCKS = NODES // P
 FEATURE_BLOCKS = FEATURES // P
+HALF = NODES // 2
+WARM_COLUMNS = 128
+WARM_MATMULS = 10
 OFFSET_COLUMNS = EDGES // 16
 
 FLOPS = 2 * ENDS * FEATURES * OUT_FEATURES * EDGES
@@ -24,26 +27,37 @@ def tile_gather_matmul_kernel(tc, table, w, b, offs, out):
     ):
         offsets = held.tile([P, ENDS * OFFSET_COLUMNS], U16, name="offsets")
         nc.sync.dma_start(offsets[:], offs)
-        nodes_first = held.tile([P, NODE_BLOCKS, FEATURES], BF16, name="nodes_first")
-        nc.sync.dma_start(nodes_first[:], table.rearrange("(a p) k -> p a k", p=P))
+        node_blocks = []
+        for a in range(NODE_BLOCKS):
+            block = held.tile([P, FEATURES], BF16, name=f"nodes{a}")
+            queue = nc.sync if a % 2 == 0 else nc.scalar
+            queue.dma_start(block[:], table[a * P : (a + 1) * P, :])
+            node_blocks.append(block)
         weights = held.tile([P, ENDS, FEATURE_BLOCKS, OUT_FEATURES], BF16, name="weights")
         nc.scalar.dma_start(weights[:], w.rearrange("t (c p) m -> p t c m", p=P))
         bias = held.tile([P, 1], F32, name="bias")
-        nc.scalar.dma_start(bias[:], b)
+        nc.sync.dma_start(bias[:], b)
 
         identity = held.tile([P, P], BF16, name="identity")
         make_identity(nc, identity[:])
 
-        windows = []
-        for c in range(FEATURE_BLOCKS):
-            flipped = psum.tile([P, NODES], BF16, name=f"flipped{c}")
-            for a in range(NODE_BLOCKS):
-                nc.tensor.transpose(
-                    flipped[:, a * P : (a + 1) * P], nodes_first[:, a, c * P : (c + 1) * P], identity[:]
-                )
-            window = held.tile([P, NODES], BF16, name=f"window{c}")
-            nc.vector.tensor_copy(window[:], flipped[:])
-            windows.append(window)
+        zeros = held.tile([P, WARM_COLUMNS], BF16, name="zeros")
+        nc.vector.memset(zeros[:], 0.0)
+        unused = psum.tile([P, WARM_COLUMNS], F32, name="unused")
+        for i in range(WARM_MATMULS):
+            nc.tensor.matmul(unused[:], zeros[:, 0:P], zeros[:], start=True, stop=True)
+
+        windows = [held.tile([P, NODES], BF16, name=f"window{c}") for c in range(FEATURE_BLOCKS)]
+        for h in range(NODES // HALF):
+            for c in range(FEATURE_BLOCKS):
+                flipped = psum.tile([P, HALF], BF16, name=f"flipped{c}{h}")
+                for j in range(HALF // P):
+                    a = h * (HALF // P) + j
+                    nc.tensor.transpose(
+                        flipped[:, j * P : (j + 1) * P], node_blocks[a][:, c * P : (c + 1) * P], identity[:]
+                    )
+                half_window = windows[c][:, h * HALF : (h + 1) * HALF]
+                nc.vector.tensor_copy(half_window, flipped[:])
 
         product = psum.tile([P, EDGES], F32, name="product")
         steps = [(c, t) for c in range(FEATURE_BLOCKS) for t in range(ENDS)]

@@ -12,8 +12,6 @@ OUT_FEATURES = 128
 NODE_BLOCKS = NODES // P
 FEATURE_BLOCKS = FEATURES // P
 HALF = NODES // 2
-WARM_COLUMNS = 128
-WARM_MATMULS = 10
 OFFSET_COLUMNS = EDGES // 16
 
 FLOPS = 2 * ENDS * FEATURES * OUT_FEATURES * EDGES
@@ -41,11 +39,6 @@ def tile_gather_matmul_kernel(tc, table, w, b, offs, out):
         identity = held.tile([P, P], BF16, name="identity")
         make_identity(nc, identity[:])
 
-        zeros = held.tile([P, WARM_COLUMNS], BF16, name="zeros")
-        nc.vector.memset(zeros[:], 0.0)
-        unused = psum.tile([P, WARM_COLUMNS], F32, name="unused")
-        for i in range(WARM_MATMULS):
-            nc.tensor.matmul(unused[:], zeros[:, 0:P], zeros[:], start=True, stop=True)
 
         windows = [held.tile([P, NODES], BF16, name=f"window{c}") for c in range(FEATURE_BLOCKS)]
         for h in range(NODES // HALF):

@@ -12,6 +12,8 @@ OUT_FEATURES = 128
 NODE_BLOCKS = NODES // P
 FEATURE_BLOCKS = FEATURES // P
 HALF = NODES // 2
+WARM_COLUMNS = 128
+WARM_MATMULS = 16
 OFFSET_COLUMNS = EDGES // 16
 
 FLOPS = 2 * ENDS * FEATURES * OUT_FEATURES * EDGES
@@ -39,6 +41,11 @@ def tile_gather_matmul_kernel(tc, table, w, b, offs, out):
         identity = held.tile([P, P], BF16, name="identity")
         make_identity(nc, identity[:])
 
+        zeros = held.tile([P, WARM_COLUMNS], BF16, name="zeros")
+        nc.vector.memset(zeros[:], 0.0)
+        unused = psum.tile([P, WARM_COLUMNS], F32, name="unused")
+        for i in range(WARM_MATMULS):
+            nc.tensor.matmul(unused[:], zeros[:, 0:P], zeros[:], start=True, stop=True)
 
         windows = [held.tile([P, NODES], BF16, name=f"window{c}") for c in range(FEATURE_BLOCKS)]
         for h in range(NODES // HALF):

@@ -13,7 +13,7 @@ NODE_BLOCKS = NODES // P
 FEATURE_BLOCKS = FEATURES // P
 HALF = NODES // 2
 WARM_COLUMNS = 128
-WARM_MATMULS = 16
+WARM_MATMULS = 10
 OFFSET_COLUMNS = EDGES // 16
 
 FLOPS = 2 * ENDS * FEATURES * OUT_FEATURES * EDGES
@@ -25,14 +25,14 @@ def tile_gather_matmul_kernel(tc, table, w, b, offs, out):
         tc.tile_pool(name="held", bufs=1) as held,
         tc.psum_pool(name="psum", bufs=1) as psum,
     ):
-        offsets = held.tile([P, ENDS * OFFSET_COLUMNS], U16, name="offsets")
-        nc.sync.dma_start(offsets[:], offs)
         node_blocks = []
         for a in range(NODE_BLOCKS):
             block = held.tile([P, FEATURES], BF16, name=f"nodes{a}")
             queue = nc.sync if a % 2 == 0 else nc.scalar
             queue.dma_start(block[:], table[a * P : (a + 1) * P, :])
             node_blocks.append(block)
+        offsets = held.tile([P, ENDS * OFFSET_COLUMNS], U16, name="offsets")
+        nc.sync.dma_start(offsets[:], offs)
         weights = held.tile([P, ENDS, FEATURE_BLOCKS, OUT_FEATURES], BF16, name="weights")
         nc.scalar.dma_start(weights[:], w.rearrange("t (c p) m -> p t c m", p=P))
         bias = held.tile([P, 1], F32, name="bias")
@@ -48,8 +48,8 @@ def tile_gather_matmul_kernel(tc, table, w, b, offs, out):
             nc.tensor.matmul(unused[:], zeros[:, 0:P], zeros[:], start=True, stop=True)
 
         windows = [held.tile([P, NODES], BF16, name=f"window{c}") for c in range(FEATURE_BLOCKS)]
-        for h in range(NODES // HALF):
-            for c in range(FEATURE_BLOCKS):
+        for c in range(FEATURE_BLOCKS):
+            for h in range(NODES // HALF):
                 flipped = psum.tile([P, HALF], BF16, name=f"flipped{c}{h}")
                 for j in range(HALF // P):
                     a = h * (HALF // P) + j

@@ -25,12 +25,12 @@ def tile_gather_matmul_kernel(tc, table, w, b, offs, out):
         tc.tile_pool(name="held", bufs=1) as held,
         tc.psum_pool(name="psum", bufs=1) as psum,
     ):
-        node_blocks = []
-        for a in range(NODE_BLOCKS):
-            block = held.tile([P, FEATURES], BF16, name=f"nodes{a}")
-            queue = nc.sync if a % 2 == 0 else nc.scalar
-            queue.dma_start(block[:], table[a * P : (a + 1) * P, :])
-            node_blocks.append(block)
+        node_halves = []
+        for h in range(NODES // HALF):
+            half = held.tile([P, HALF // P, FEATURES], BF16, name=f"nodes{h}")
+            queue = nc.sync if h == 0 else nc.scalar
+            queue.dma_start(half[:], table[h * HALF : (h + 1) * HALF, :].rearrange("(j p) k -> p j k", p=P))
+            node_halves.append(half)
         offsets = held.tile([P, ENDS * OFFSET_COLUMNS], U16, name="offsets")
         nc.sync.dma_start(offsets[:], offs)
         weights = held.tile([P, ENDS, FEATURE_BLOCKS, OUT_FEATURES], BF16, name="weights")
@@ -52,9 +52,8 @@ def tile_gather_matmul_kernel(tc, table, w, b, offs, out):
             for h in range(NODES // HALF):
                 flipped = psum.tile([P, HALF], BF16, name=f"flipped{c}{h}")
                 for j in range(HALF // P):
-                    a = h * (HALF // P) + j
                     nc.tensor.transpose(
-                        flipped[:, j * P : (j + 1) * P], node_blocks[a][:, c * P : (c + 1) * P], identity[:]
+                        flipped[:, j * P : (j + 1) * P], node_halves[h][:, j, c * P : (c + 1) * P], identity[:]
                     )
                 half_window = windows[c][:, h * HALF : (h + 1) * HALF]
                 nc.vector.tensor_copy(half_window, flipped[:])

@@ -12,8 +12,10 @@ OUT_FEATURES = 128
 NODE_BLOCKS = NODES // P
 FEATURE_BLOCKS = FEATURES // P
 HALF = NODES // 2
-WARM_COLUMNS = 128
-WARM_MATMULS = 10
+QUADRANT = 32
+QUADRANTS = P // QUADRANT
+WARM_COLUMNS = 256
+WARM_ROUNDS = 5
 OFFSET_COLUMNS = EDGES // 16
 
 FLOPS = 2 * ENDS * FEATURES * OUT_FEATURES * EDGES
@@ -41,11 +43,18 @@ def tile_gather_matmul_kernel(tc, table, w, b, offs, out):
         identity = held.tile([P, P], BF16, name="identity")
         make_identity(nc, identity[:])
 
-        zeros = held.tile([P, WARM_COLUMNS], BF16, name="zeros")
+        zeros = held.tile([P, QUADRANT], BF16, name="zeros")
         nc.vector.memset(zeros[:], 0.0)
         unused = psum.tile([P, WARM_COLUMNS], F32, name="unused")
-        for i in range(WARM_MATMULS):
-            nc.tensor.matmul(unused[:], zeros[:, 0:P], zeros[:], start=True, stop=True)
+        for i in range(WARM_ROUNDS):
+            for q in range(QUADRANTS):
+                nc.tensor.matmul(
+                    unused[q * QUADRANT : (q + 1) * QUADRANT, :],
+                    zeros[:],
+                    zeros[:, 0:1].to_broadcast([P, WARM_COLUMNS]),
+                    start=True,
+                    stop=True,
+                )
 
         windows = [held.tile([P, NODES], BF16, name=f"window{c}") for c in range(FEATURE_BLOCKS)]
         for c in range(FEATURE_BLOCKS):

@@ -26,6 +26,7 @@ def tile_gather_matmul_kernel(tc, table, w, b, offs, out):
     with (
         tc.tile_pool(name="held", bufs=1) as held,
         tc.psum_pool(name="psum", bufs=1) as psum,
+        tc.psum_pool(name="turns", bufs=6) as turns,
     ):
         node_halves = []
         for h in range(NODES // HALF):
@@ -58,14 +59,11 @@ def tile_gather_matmul_kernel(tc, table, w, b, offs, out):
 
         windows = [held.tile([P, NODES], BF16, name=f"window{c}") for c in range(FEATURE_BLOCKS)]
         for c in range(FEATURE_BLOCKS):
-            for h in range(NODES // HALF):
-                flipped = psum.tile([P, HALF], BF16, name=f"flipped{c}{h}")
-                for j in range(HALF // P):
-                    nc.tensor.transpose(
-                        flipped[:, j * P : (j + 1) * P], node_halves[h][:, j, c * P : (c + 1) * P], identity[:]
-                    )
-                half_window = windows[c][:, h * HALF : (h + 1) * HALF]
-                nc.vector.tensor_copy(half_window, flipped[:])
+            for n in range(NODE_BLOCKS):
+                flipped = turns.tile([P, P], BF16, name="flipped")
+                h, j = divmod(n, HALF // P)
+                nc.tensor.transpose(flipped[:], node_halves[h][:, j, c * P : (c + 1) * P], identity[:])
+                nc.vector.tensor_copy(windows[c][:, n * P : (n + 1) * P], flipped[:])
 
         product = psum.tile([P, EDGES], F32, name="product")
         steps = [(c, t) for c in range(FEATURE_BLOCKS) for t in range(ENDS)]

@@ -37,7 +37,7 @@ def tile_gather_matmul_kernel(tc, table, w, b, offs, out):
         offsets = held.tile([P, ENDS * OFFSET_COLUMNS], U16, name="offsets")
         nc.sync.dma_start(offsets[:], offs)
         weights = held.tile([P, ENDS, FEATURE_BLOCKS, OUT_FEATURES], BF16, name="weights")
-        nc.scalar.dma_start(weights[:], w.rearrange("t (c p) m -> p t c m", p=P))
+        nc.scalar.dma_start(weights[:], w.rearrange("t (p c) m -> p t c m", p=P))
         bias = held.tile([P, 1], F32, name="bias")
         nc.sync.dma_start(bias[:], b)
 
@@ -62,7 +62,7 @@ def tile_gather_matmul_kernel(tc, table, w, b, offs, out):
             for n in range(NODE_BLOCKS):
                 flipped = turns.tile([P, P], BF16, name="flipped")
                 h, j = divmod(n, HALF // P)
-                nc.tensor.transpose(flipped[:], node_halves[h][:, j, c * P : (c + 1) * P], identity[:])
+                nc.tensor.transpose(flipped[:], node_halves[h][:, j, c:FEATURES:FEATURE_BLOCKS], identity[:])
                 nc.vector.tensor_copy(windows[c][:, n * P : (n + 1) * P], flipped[:])
 
         product = psum.tile([P, EDGES], F32, name="product")

import concourse.mybir as mybir
from concourse.masks import make_identity

BF16, F32, U16 = mybir.dt.bfloat16, mybir.dt.float32, mybir.dt.uint16

P = 128
NODES = 512
FEATURES = 256
ENDS = 2
EDGES = 128
OUT_FEATURES = 128
NODE_BLOCKS = NODES // P
FEATURE_BLOCKS = FEATURES // P
HALF = NODES // 2
QUADRANT = 32
QUADRANTS = P // QUADRANT
WARM_COLUMNS = 256
WARM_ROUNDS = 5
OFFSET_COLUMNS = EDGES // 16

FLOPS = 2 * ENDS * FEATURES * OUT_FEATURES * EDGES


def tile_gather_matmul_kernel(tc, table, w, b, offs, out):
    nc = tc.nc
    with (
        tc.tile_pool(name="held", bufs=1) as held,
        tc.psum_pool(name="psum", bufs=1) as psum,
        tc.psum_pool(name="turns", bufs=6) as turns,
    ):
        node_halves = []
        for h in range(NODES // HALF):
            half = held.tile([P, HALF // P, FEATURES], BF16, name=f"nodes{h}")
            queue = nc.sync if h == 0 else nc.scalar
            queue.dma_start(half[:], table[h * HALF : (h + 1) * HALF, :].rearrange("(j p) k -> p j k", p=P))
            node_halves.append(half)
        offsets = held.tile([P, ENDS * OFFSET_COLUMNS], U16, name="offsets")
        nc.sync.dma_start(offsets[:], offs)
        weights = held.tile([P, ENDS, FEATURE_BLOCKS, OUT_FEATURES], BF16, name="weights")
        nc.scalar.dma_start(weights[:], w.rearrange("t (p c) m -> p t c m", p=P))
        bias = held.tile([P, 1], F32, name="bias")
        nc.sync.dma_start(bias[:], b)

        identity = held.tile([P, P], BF16, name="identity")
        make_identity(nc, identity[:])

        zeros = held.tile([P, QUADRANT], BF16, name="zeros")
        nc.vector.memset(zeros[:], 0.0)
        unused = psum.tile([P, WARM_COLUMNS], F32, name="unused")
        for i in range(WARM_ROUNDS):
            for q in range(QUADRANTS):
                nc.tensor.matmul(
                    unused[q * QUADRANT : (q + 1) * QUADRANT, :],
                    zeros[:],
                    zeros[:, 0:1].to_broadcast([P, WARM_COLUMNS]),
                    start=True,
                    stop=True,
                )

        windows = [held.tile([P, NODES], BF16, name=f"window{c}") for c in range(FEATURE_BLOCKS)]
        for c in range(FEATURE_BLOCKS):
            for n in range(NODE_BLOCKS):
                flipped = turns.tile([P, P], BF16, name="flipped")
                h, j = divmod(n, HALF // P)
                nc.tensor.transpose(flipped[:], node_halves[h][:, j, c:FEATURES:FEATURE_BLOCKS], identity[:])
                nc.vector.tensor_copy(windows[c][:, n * P : (n + 1) * P], flipped[:])

        product = psum.tile([P, EDGES], F32, name="product")
        steps = [(c, t) for c in range(FEATURE_BLOCKS) for t in range(ENDS)]
        for step, (c, t) in enumerate(steps):
            picked = windows[c][:].indirect(offsets[:, t * OFFSET_COLUMNS : (t + 1) * OFFSET_COLUMNS])
            nc.tensor.matmul(
                product[:], weights[:, t, c, :], picked, start=(step == 0), stop=(step == len(steps) - 1)
            )

        result = held.tile([P, EDGES], F32, name="result")
        nc.vector.tensor_scalar_add(result[:], product[:], bias[:, 0:1])
        nc.sync.dma_start(out, result[:])
